import numpy as np
import ml_dtypes


def mxq(x, axis, fmt="e4m3"):
    dtype, down = {"e4m3": (ml_dtypes.float8_e4m3fn, 7), "e5m2": (ml_dtypes.float8_e5m2, 14)}[fmt]
    v = np.moveaxis(np.asarray(x, np.float32).astype(ml_dtypes.bfloat16).astype(np.float64), axis, -1)
    blocks = v.reshape(v.shape[:-1] + (-1, 32))
    amax = np.abs(blocks).max(-1, keepdims=True)
    byte = np.maximum(np.where(amax > 0, np.frexp(amax)[1] - 1 + 127, 0) - down, 1)
    scale = np.exp2(byte - 127.0)
    codes = (blocks / scale).astype(np.float32).astype(dtype).astype(np.float64)
    return np.moveaxis((codes * scale).reshape(v.shape), -1, axis)


WIDE = False


def mx_kscale(k):
    if not WIDE:
        return np.ones(k)
    levels = np.array([10, -10, 5, -5, 0])
    if k % 512:
        return np.exp2(np.random.permutation(np.resize(levels, k // 32))).repeat(32)
    a = np.empty((k // 512, 16))
    for p in range(k // 512):
        a[p, :8] = np.random.permutation(np.resize(levels, 8))
        for g in range(8):
            far = levels[np.abs(levels - a[p, g]) >= 10]
            a[p, g + 8] = far[np.random.randint(len(far))]
    return np.exp2(a.ravel()).repeat(32)


BF16 = ml_dtypes.bfloat16


def bf(x):
    return np.asarray(x, np.float32).astype(BF16)


def f64(x):
    return np.asarray(x).astype(np.float64)

def planes(Y):
    n, m = Y.shape
    b = f64(bf(Y)).reshape(n // 32, 32, m)
    amax = np.abs(b).max(1)
    byte = np.clip(np.where(amax > 0, np.frexp(amax)[1] - 1 + 127 - 7, 1), 1, 254)
    codes = (b * np.exp2(127.0 - byte)[:, None, :]).reshape(n, m).astype(np.float32).astype(ml_dtypes.float8_e4m3fn).view(np.uint8)
    words = codes.reshape(n // 512, 128, 4, m).transpose(0, 1, 3, 2)
    return np.ascontiguousarray(words), np.ascontiguousarray(byte.astype(np.uint8).reshape(n // 512, 16, m))


C, R, B = 2048, 512, 1024

def setup_inputs():
    s = mx_kscale(C)
    t = mx_kscale(R)
    means = bf(np.random.randn(C, B) * s[:, None])
    w_reduce = bf(np.random.randn(R, C) / np.sqrt(C) * t[:, None] / s[None, :])
    b_reduce = bf(0.3 * np.random.randn(R) * t)
    w_expand = bf(2.0 * np.random.randn(C, R) / np.sqrt(R) / t[None, :])
    b_expand = bf(0.5 * np.random.randn(C))
    gain = bf(np.exp(0.8 * np.random.randn(C)) / s)
    return {"means": means, "w_reduce": w_reduce, "b_reduce": b_reduce,
            "w_expand": w_expand, "b_expand": b_expand, "gain": gain}

def reference(means, w_reduce, b_reduce, w_expand, b_expand, gain):
    z = f64(means)
    a = mxq(f64(w_reduce), 1, "e4m3") @ mxq(z, 0, "e4m3")
    h = np.maximum(a + f64(b_reduce)[:, None], 0.0)
    e = mxq(f64(w_expand), 1, "e4m3") @ mxq(h, 0, "e4m3")
    gate = 1.0 / (1.0 + np.exp(-(e + f64(b_expand)[:, None])))
    y = gate * z * f64(gain)[:, None]
    Y = y
    words, scales = planes(Y)
    return y, words, scales

from contextlib import ExitStack

import concourse.mybir as mybir
from concourse.masks import make_identity

C, R, B = 2048, 512, 1024
FLOPS = 2 * 2 * C * R * B

F32 = mybir.dt.float32
BF16 = mybir.dt.bfloat16
U32 = mybir.dt.uint32
I32 = mybir.dt.int32
U8 = mybir.dt.uint8
FP8X4 = mybir.dt.float8_e4m3fn_x4
ACT = mybir.ActivationFunctionType
ALU = mybir.AluOpType

P = 128
N = 512
ORDER = [
    ('setup',),
    ('load', 'Z00'),
    ('load', 'WR0'),
    ('load', 'Z10'),
    ('load', 'WR1'),
    ('vec_load',),
    ('load', 'Z20'),
    ('load', 'WR2'),
    ('load', 'Z30'),
    ('load', 'WR3'),
    ('load', 'Z01'),
    ('load', 'WE0'),
    ('load', 'Z11'),
    ('load', 'WE1'),
    ('load', 'Z21'),
    ('load', 'WE2'),
    ('load', 'Z31'),
    ('load', 'WE3'),
    ('il', 'Z00', False, 0, 256),
    ('il', 'Z00', True, 256, 512),
    ('w_t', 'WR0', 0, 0),
    ('w_t', 'WR0', 1, 1),
    ('quant', 'Z00', 0, 512),
    ('w_ev', 'WR0', 0),
    ('w_ev', 'WR0', 1),
    ('il', 'Z10', False, 0, 384),
    ('il', 'Z10', True, 384, 512),
    ('w_t', 'WR1', 0, 2),
    ('w_t', 'WR1', 1, 3),
    ('quant', 'WR0', 0, 512),
    ('quant', 'Z10', 0, 512),
    ('w_ev', 'WR1', 0),
    ('w_ev', 'WR1', 1),
    ('p1', 0, 0, 0, True, False),
    ('p1', 0, 0, 1, False, False),
    ('vec_t', 0),
    ('il', 'Z20', False, 0, 384),
    ('il', 'Z20', True, 384, 512),
    ('w_t', 'WR2', 0, 1),
    ('w_t', 'WR2', 1, 2),
    ('quant', 'WR1', 0, 512),
    ('quant', 'Z20', 0, 512),
    ('w_ev', 'WR2', 0),
    ('w_ev', 'WR2', 1),
    ('p1', 0, 1, 0, True, False),
    ('p1', 0, 1, 1, False, False),
    ('p1', 0, 0, 2, False, False),
    ('p1', 0, 1, 2, False, False),
    ('vec_ev',),
    ('il', 'Z30', False, 0, 448),
    ('il', 'Z30', True, 448, 512),
    ('w_t', 'WR3', 0, 3),
    ('w_t', 'WR3', 1, 0),
    ('quant', 'WR2', 0, 512),
    ('quant', 'Z30', 0, 512),
    ('w_ev', 'WR3', 0),
    ('w_ev', 'WR3', 1),
    ('p1', 0, 2, 0, True, False),
    ('p1', 0, 2, 1, False, False),
    ('p1', 0, 2, 2, False, False),
    ('p1', 0, 0, 3, False, True),
    ('p1', 0, 1, 3, False, True),
    ('p1', 0, 2, 3, False, True),
    ('il', 'Z01', False, 0, 512),
    ('quant', 'WR3', 0, 512),
    ('p1', 0, 3, 0, True, False),
    ('p1', 0, 3, 1, False, False),
    ('p1', 0, 3, 2, False, False),
    ('p1', 0, 3, 3, False, True),
    ('w_t', 'WE0', 0, 1),
    ('w_t', 'WE0', 1, 2),
    ('relu', 0, 0),
    ('relu', 0, 1),
    ('relu', 0, 2),
    ('relu', 0, 3),
    ('w_ev', 'WE0', 0),
    ('w_ev', 'WE0', 1),
    ('w_t', 'WE1', 0, 3),
    ('w_t', 'WE1', 1, 0),
    ('quant', 'Z01', 0, 512),
    ('il', 'Z11', False, 0, 512),
    ('il', 'H0', False, 0, 512),
    ('quant', 'WE0', 0, 512),
    ('quant', 'H0', 0, 512),
    ('w_ev', 'WE1', 0),
    ('w_ev', 'WE1', 1),
    ('w_t', 'WE2', 0, 1),
    ('w_t', 'WE2', 1, 2),
    ('p2', 0, 0, 0, 0, 512, 3),
    ('p2', 0, 0, 1, 0, 512, 0),
    ('quant', 'Z11', 0, 512),
    ('il', 'Z21', False, 0, 320),
    ('il', 'Z21', True, 320, 512),
    ('quant', 'WE1', 0, 512),
    ('w_ev', 'WE2', 0),
    ('w_ev', 'WE2', 1),
    ('p2', 0, 0, 2, 0, 512, 1),
    ('p2', 0, 0, 3, 0, 512, 2),
    ('quant', 'Z21', 0, 512),
    ('il', 'Z31', False, 0, 416),
    ('sig', 0, 0, 0, 0, 512),
    ('stt', 0, 0, 0, 0, 512),
    ('sig', 0, 0, 1, 0, 512),
    ('stt', 0, 0, 1, 0, 512),
    ('w_t', 'WE3', 0, 3),
    ('w_t', 'WE3', 1, 0),
    ('quant', 'WE2', 0, 512),
    ('sig', 0, 0, 2, 0, 512),
    ('stt', 0, 0, 2, 0, 512),
    ('p2', 1, 0, 0, 0, 512, 1),
    ('sig', 0, 0, 3, 0, 512),
    ('stt', 0, 0, 3, 0, 512),
    ('p2', 1, 0, 1, 0, 512, 2),
    ('w_ev', 'WE3', 0),
    ('w_ev', 'WE3', 1),
    ('il', 'Z31', True, 416, 512),
    ('p2', 1, 0, 2, 0, 512, 3),
    ('p2', 1, 0, 3, 0, 512, 0),
    ('sy', 0, 0, 0, 4, 0, 512),
    ('p1', 1, 0, 0, True, False),
    ('p1', 1, 1, 0, True, False),
    ('p1', 1, 2, 0, True, False),
    ('p1', 1, 3, 0, True, False),
    ('p1', 1, 0, 1, False, False),
    ('p1', 1, 1, 1, False, False),
    ('p1', 1, 2, 1, False, False),
    ('p1', 1, 3, 1, False, False),
    ('quant', 'Z31', 0, 512),
    ('il', 'Y00', False, 0, 288),
    ('sig', 1, 0, 0, 0, 512),
    ('stt', 1, 0, 0, 0, 512),
    ('p2', 2, 0, 0, 0, 512, 1),
    ('sig', 1, 0, 1, 0, 512),
    ('stt', 1, 0, 1, 0, 512),
    ('p2', 2, 0, 1, 0, 512, 2),
    ('quant', 'WE3', 0, 512),
    ('sig', 1, 0, 2, 0, 512),
    ('stt', 1, 0, 2, 0, 512),
    ('p2', 2, 0, 2, 0, 512, 3),
    ('sig', 1, 0, 3, 0, 512),
    ('stt', 1, 0, 3, 0, 512),
    ('p2', 2, 0, 3, 0, 512, 0),
    ('sy', 1, 0, 0, 4, 0, 512),
    ('il', 'Y00', True, 288, 512),
    ('p1', 1, 0, 2, False, False),
    ('p1', 1, 1, 2, False, False),
    ('p1', 1, 2, 2, False, False),
    ('p1', 1, 3, 2, False, False),
    ('p1', 1, 0, 3, False, True),
    ('p1', 1, 1, 3, False, True),
    ('p1', 1, 2, 3, False, True),
    ('p1', 1, 3, 3, False, True),
    ('quant', 'Y00', 0, 512),
    ('sw', 0, 0, 0, 512),
    ('il', 'Y10', False, 0, 320),
    ('sig', 2, 0, 0, 0, 512),
    ('stt', 2, 0, 0, 0, 512),
    ('p2', 3, 0, 0, 0, 512, 1),
    ('sig', 2, 0, 1, 0, 512),
    ('stt', 2, 0, 1, 0, 512),
    ('p2', 3, 0, 1, 0, 512, 2),
    ('sig', 2, 0, 2, 0, 512),
    ('stt', 2, 0, 2, 0, 512),
    ('p2', 3, 0, 2, 0, 512, 3),
    ('sig', 2, 0, 3, 0, 512),
    ('stt', 2, 0, 3, 0, 512),
    ('p2', 3, 0, 3, 0, 512, 0),
    ('sy', 2, 0, 0, 4, 0, 512),
    ('il', 'Y10', True, 320, 512),
    ('relu', 1, 0),
    ('relu', 1, 1),
    ('relu', 1, 2),
    ('relu', 1, 3),
    ('quant', 'Y10', 0, 512),
    ('sw', 1, 0, 0, 512),
    ('il', 'Y20', False, 0, 256),
    ('il', 'H1', False, 0, 384),
    ('sig', 3, 0, 0, 0, 512),
    ('stt', 3, 0, 0, 0, 512),
    ('il', 'H1', True, 384, 512),
    ('sig', 3, 0, 1, 0, 512),
    ('stt', 3, 0, 1, 0, 512),
    ('quant', 'H1', 0, 512),
    ('sig', 3, 0, 2, 0, 512),
    ('stt', 3, 0, 2, 0, 512),
    ('sig', 3, 0, 3, 0, 512),
    ('stt', 3, 0, 3, 0, 512),
    ('p2', 0, 1, 0, 0, 512, 1),
    ('p2', 0, 1, 1, 0, 512, 2),
    ('p2', 0, 1, 2, 0, 512, 3),
    ('p2', 0, 1, 3, 0, 512, 0),
    ('sy', 3, 0, 0, 4, 0, 512),
    ('il', 'Y20', True, 256, 512),
    ('quant', 'Y20', 0, 512),
    ('sw', 2, 0, 0, 512),
    ('il', 'Y30', False, 0, 288),
    ('sig', 0, 1, 0, 0, 512),
    ('stt', 0, 1, 0, 0, 512),
    ('p2', 1, 1, 0, 0, 512, 1),
    ('sig', 0, 1, 1, 0, 512),
    ('stt', 0, 1, 1, 0, 512),
    ('p2', 1, 1, 1, 0, 512, 2),
    ('sig', 0, 1, 2, 0, 512),
    ('stt', 0, 1, 2, 0, 512),
    ('p2', 1, 1, 2, 0, 512, 3),
    ('sig', 0, 1, 3, 0, 512),
    ('stt', 0, 1, 3, 0, 512),
    ('p2', 1, 1, 3, 0, 512, 0),
    ('sy', 0, 1, 0, 4, 0, 512),
    ('il', 'Y30', True, 288, 512),
    ('quant', 'Y30', 0, 512),
    ('sw', 3, 0, 0, 512),
    ('ss', 0),
    ('il', 'Y01', False, 0, 256),
    ('sig', 1, 1, 0, 0, 512),
    ('stt', 1, 1, 0, 0, 512),
    ('p2', 2, 1, 0, 0, 512, 1),
    ('sig', 1, 1, 1, 0, 512),
    ('stt', 1, 1, 1, 0, 512),
    ('p2', 2, 1, 1, 0, 512, 2),
    ('sig', 1, 1, 2, 0, 512),
    ('stt', 1, 1, 2, 0, 512),
    ('p2', 2, 1, 2, 0, 512, 3),
    ('sig', 1, 1, 3, 0, 512),
    ('stt', 1, 1, 3, 0, 512),
    ('p2', 2, 1, 3, 0, 512, 0),
    ('sy', 1, 1, 0, 4, 0, 512),
    ('il', 'Y01', True, 256, 512),
    ('quant', 'Y01', 0, 512),
    ('sw', 0, 1, 0, 512),
    ('il', 'Y11', False, 0, 160),
    ('sig', 2, 1, 0, 0, 512),
    ('stt', 2, 1, 0, 0, 512),
    ('p2', 3, 1, 0, 0, 256, 1),
    ('sig', 2, 1, 1, 0, 512),
    ('stt', 2, 1, 1, 0, 512),
    ('p2', 3, 1, 1, 0, 256, 2),
    ('sig', 2, 1, 2, 0, 512),
    ('stt', 2, 1, 2, 0, 512),
    ('p2', 3, 1, 2, 0, 256, 3),
    ('sig', 2, 1, 3, 0, 512),
    ('stt', 2, 1, 3, 0, 512),
    ('p2', 3, 1, 3, 0, 256, 0),
    ('sy', 2, 1, 0, 4, 0, 512),
    ('il', 'Y11', True, 160, 512),
    ('quant', 'Y11', 0, 512),
    ('sw', 1, 1, 0, 512),
    ('il', 'Y21', False, 0, 256),
    ('sig', 3, 1, 0, 0, 256),
    ('stt', 3, 1, 0, 0, 256),
    ('p2', 3, 1, 0, 256, 512, 1),
    ('sig', 3, 1, 1, 0, 256),
    ('stt', 3, 1, 1, 0, 256),
    ('p2', 3, 1, 1, 256, 512, 2),
    ('sig', 3, 1, 2, 0, 256),
    ('stt', 3, 1, 2, 0, 256),
    ('p2', 3, 1, 2, 256, 512, 3),
    ('sig', 3, 1, 3, 0, 256),
    ('stt', 3, 1, 3, 0, 256),
    ('p2', 3, 1, 3, 256, 512, 0),
    ('sy', 3, 1, 0, 4, 0, 256),
    ('il', 'Y21', True, 256, 512),
    ('quant', 'Y21', 0, 512),
    ('sw', 2, 1, 0, 512),
    ('sig', 3, 1, 0, 256, 512),
    ('stt', 3, 1, 0, 256, 512),
    ('sig', 3, 1, 1, 256, 512),
    ('stt', 3, 1, 1, 256, 512),
    ('sig', 3, 1, 2, 256, 512),
    ('stt', 3, 1, 2, 256, 512),
    ('sig', 3, 1, 3, 256, 512),
    ('stt', 3, 1, 3, 256, 512),
    ('sy', 3, 1, 0, 4, 256, 512),
    ('il', 'Y31', True, 0, 256),
    ('il', 'Y31', False, 256, 416),
    ('quant', 'Y31', 0, 256),
    ('sw', 3, 1, 0, 256),
    ('il', 'Y31', True, 416, 512),
    ('quant', 'Y31', 256, 512),
    ('sw', 3, 1, 256, 512),
    ('ss', 1),
]


def tile_squeeze_excitation_gated_means_h3_kernel(
    tc, means, w_reduce, b_reduce, w_expand, b_expand, gain, out_0, out_1, out_2
):
    nc = tc.nc
    with ExitStack() as ctx:
        keep = ctx.enter_context(tc.tile_pool(name="keep", bufs=1))
        stage = ctx.enter_context(tc.tile_pool(name="stage", bufs=3))
        psum = ctx.enter_context(tc.psum_pool(name="psum", bufs=1))
        ctx.enter_context(tc.manual_schedule())

        tiles = {}
        out_words = out_1.rearrange("g p m t -> g p (m t)").bitcast(I32)
        out_scales = out_2.bitcast(I32)

        def cols(h):
            return slice(h * N, (h + 1) * N)

        def load(name):
            raw = keep.tile([P, 4, N], BF16, name="raw" + name, align_bytes=64)
            i = int(name[-1])
            if name.startswith("WR"):
                src = w_reduce.rearrange("(m t) (g k) -> t m g k", t=4, g=4)[i]
            elif name.startswith("WE"):
                src = w_expand.rearrange("(g m t) k -> g m t k", t=4, g=4)[i]
            else:
                g = int(name[1])
                src = means.rearrange("(g p t) n -> g p t n", t=4, g=4)[g][:, :, cols(i)]
            nc.sync.dma_start(out=raw[:], in_=src)
            tiles["raw" + name] = raw

        ident = keep.tile([P, P], F32, name="ident")
        vec_rows = keep.tile([P, N], BF16, name="vec_rows")
        vec = keep.tile([P, 9, 4], F32, name="vec")

        def setup():
            make_identity(nc, ident[:])
            words = vec_rows[:].bitcast(F32)
            for u in (0, 1):
                nc.scalar.activation(out=words[:, u * P:(u + 1) * P], in_=ident[:], func=ACT.Sigmoid)

        def vec_load():
            nc.sync.dma_start(out=vec_rows[0:4, :], in_=b_expand.rearrange("(g k) -> g k", g=4))
            nc.sync.dma_start(out=vec_rows[4:8, :], in_=gain.rearrange("(g k) -> g k", g=4))
            nc.sync.dma_start(out=vec_rows[8:9, :], in_=b_reduce.rearrange("(g k) -> g k", g=1))

        def vec_t(bank):
            ps = psum.tile([P, 4, P], F32, name="rot%d" % bank)
            words = vec_rows[:].bitcast(F32)
            for u in (0, 1):
                nc.tensor.transpose(ps[:, u, :], words[:, u:2 * P:2], ident[:])
            tiles["psvec"] = ps

        def vec_ev():
            src = tiles["psvec"][:, 0:2, :].bitcast(BF16)[:, :, 0:18]
            nc.vector.tensor_copy(
                out=vec[:].rearrange("p r (u e) -> p r u e", u=2),
                in_=src.rearrange("p u (r e) -> p r u e", e=2),
            )

        def w_t(name, b, bank):
            ps = psum.tile([P, 4, P], F32, name="rot%d" % bank)
            words = tiles["raw" + name][:].rearrange("p j k -> p (j k)").bitcast(F32)
            for jj in (0, 1):
                j = 2 * b + jj
                for u in (0, 1):
                    nc.tensor.transpose(ps[:, 2 * jj + u, :], words[:, 256 * j + u:256 * (j + 1):2], ident[:])
            tiles["ps" + name + str(b)] = ps

        def grouped(name, tag):
            if "grp" + name not in tiles:
                tiles["grp" + name] = stage.tile([P, N * 4], BF16, name=tag, align_bytes=64)
            return tiles["grp" + name]

        def w_ev(name, b):
            dst = grouped(name, "wgrp")[:].bitcast(F32)[:, 512 * b:512 * (b + 1)]
            nc.scalar.copy(
                out=dst.rearrange("p (j m u) -> p j m u", j=2, u=2),
                in_=tiles["ps" + name + str(b)][:].rearrange("p (j u) m -> p j m u", u=2),
            )

        def quant(name, c0, c1):
            if "codes" + name not in tiles:
                tiles["codes" + name] = keep.tile([P, N], U32, name="codes" + name, align_bytes=64)
            codes = tiles["codes" + name]
            if name.startswith("Y"):
                g, h = int(name[1]), int(name[2])
                if "ysc%d" % h not in tiles:
                    tiles["ysc%d" % h] = keep.tile([P, N], U8, name="ysc%d" % h, align_bytes=64)
                sc = tiles["ysc%d" % h][4 * g:P, c0:c1]
            else:
                tiles["sc" + name] = keep.tile([P, N], U8, name="sc" + name, align_bytes=64)
                sc = tiles["sc" + name][:]
            nc.vector.quantize_mx(out=codes[:, c0:c1].bitcast(FP8X4), scales=sc,
                                  in_=tiles["grp" + name][:, 4 * c0:4 * c1])

        def interleave(name, on_scalar, lo, hi):
            dst = grouped(name, name[0] + "grp")[:, 4 * lo:4 * hi].rearrange("p (c i t) -> p c t i", i=4, t=4)
            src = tiles["raw" + name][:, :, lo:hi].rearrange("p t (c i) -> p c t i", i=4)
            if on_scalar:
                nc.scalar.copy(out=dst, in_=src)
            else:
                nc.vector.tensor_copy(out=dst, in_=src)

        def mm(acc, w, j, x, start, stop, c0=0, c1=N):
            nc.tensor.matmul_mx(
                out=acc,
                lhsT=tiles["codes" + w][:, j * P:(j + 1) * P].bitcast(FP8X4),
                lhsT_scale=tiles["sc" + w][:, j * P:(j + 1) * P],
                rhs=tiles["codes" + x][:, c0:c1].bitcast(FP8X4),
                rhs_scale=tiles["sc" + x][:, c0:c1],
                start=start,
                stop=stop,
            )

        def p1(h, t, g, first, last):
            if first:
                tiles["acc%d%d" % (h, t)] = psum.tile([P, N], F32, name="acc%d" % t)
            mm(tiles["acc%d%d" % (h, t)][:], "WR%d" % t, g, "Z%d%d" % (g, h), first, last)

        def relu(h, t):
            if "rawH%d" % h not in tiles:
                tiles["rawH%d" % h] = keep.tile([P, 4, N], BF16, name="rawH%d" % h)
            nc.scalar.activation(out=tiles["rawH%d" % h][:, t, :], in_=tiles["acc%d%d" % (h, t)][:],
                                 func=ACT.Relu, bias=vec[:, 8, t:t + 1])

        def p2(g, h, t, c0, c1, bank):
            ps = psum.tile([P, N], F32, name="rot%d" % bank)
            mm(ps[:, c0:c1], "WE%d" % g, t, "H%d" % h, True, True, c0, c1)
            tiles["e", g, h, t, c0] = ps

        def sig(g, h, t, c0, c1):
            gate = stage.tile([P, N], F32, name="gate", bufs=6)
            nc.scalar.activation(out=gate[:, c0:c1], in_=tiles["e", g, h, t, c0][:, c0:c1],
                                 func=ACT.Sigmoid, bias=vec[:, g, t:t + 1])
            tiles["gate", g, h, t, c0] = gate

        def stt(g, h, t, c0, c1):
            name = "rawY%d%d" % (g, h)
            if name not in tiles:
                tiles[name] = stage.tile([P, 4, N], F32, name="y32", bufs=5)
            nc.vector.scalar_tensor_tensor(
                out=tiles[name][:, t, c0:c1], in0=tiles["gate", g, h, t, c0][:, c0:c1], scalar=vec[:, 4 + g, t:t + 1],
                in1=tiles["rawZ%d%d" % (g, h)][:, t, c0:c1], op0=ALU.mult, op1=ALU.mult)

        def store_y(g, h, t0, t1, c0, c1):
            dst = out_0.rearrange("(g p t) n -> g p t n", t=4, g=4)[g][:, t0:t1, h * N + c0:h * N + c1]
            nc.sync.dma_start(out=dst, in_=tiles["rawY%d%d" % (g, h)][:, t0:t1, c0:c1])

        def store_w(g, h, c0, c1):
            nc.sync.dma_start(out=out_words[g][:, h * N + c0:h * N + c1],
                              in_=tiles["codesY%d%d" % (g, h)][:, c0:c1].bitcast(I32))

        def store_s(h):
            for q in range(4):
                eng = nc.scalar if h == 1 and q < 2 else nc.sync
                eng.dma_start(
                    out=out_scales[:, 4 * q:4 * q + 4, h * 128:(h + 1) * 128],
                    in_=tiles["ysc%d" % h][32 * q:32 * q + 16, :].bitcast(I32))

        steps = {"load": load, "setup": setup, "vec_load": vec_load, "vec_t": vec_t, "vec_ev": vec_ev, "w_t": w_t, "w_ev": w_ev,
                 "quant": quant, "il": interleave, "p1": p1, "relu": relu, "p2": p2, "sig": sig, "stt": stt,
                 "sy": store_y, "sw": store_w, "ss": store_s}
        for step in ORDER:
            steps[step[0]](*step[1:])
